import numpy as np
import ml_dtypes


def mxq(x, axis, fmt="e4m3"):
    dtype, down = {"e4m3": (ml_dtypes.float8_e4m3fn, 7), "e5m2": (ml_dtypes.float8_e5m2, 14)}[fmt]
    v = np.moveaxis(np.asarray(x, np.float32).astype(ml_dtypes.bfloat16).astype(np.float64), axis, -1)
    blocks = v.reshape(v.shape[:-1] + (-1, 32))
    amax = np.abs(blocks).max(-1, keepdims=True)
    byte = np.maximum(np.where(amax > 0, np.frexp(amax)[1] - 1 + 127, 0) - down, 1)
    scale = np.exp2(byte - 127.0)
    codes = (blocks / scale).astype(np.float32).astype(dtype).astype(np.float64)
    return np.moveaxis((codes * scale).reshape(v.shape), -1, axis)


WIDE = False


def mx_kscale(k):
    if not WIDE:
        return np.ones(k)
    levels = np.array([10, -10, 5, -5, 0])
    if k % 512:
        return np.exp2(np.random.permutation(np.resize(levels, k // 32))).repeat(32)
    a = np.empty((k // 512, 16))
    for p in range(k // 512):
        a[p, :8] = np.random.permutation(np.resize(levels, 8))
        for g in range(8):
            far = levels[np.abs(levels - a[p, g]) >= 10]
            a[p, g + 8] = far[np.random.randint(len(far))]
    return np.exp2(a.ravel()).repeat(32)


def f64(x):
    return np.asarray(x).astype(np.float64)


def striped(idx):
    return np.tile(np.asarray(idx).reshape(-1, 16).T, (8, 1)).astype(np.uint16)


def unstriped(offs):
    return offs[:16].T.reshape(-1).astype(np.int64)


E2M1 = np.array([0.0, 0.5, 1.0, 1.5, 2.0, 3.0, 4.0, 6.0, -0.0, -0.5, -1.0, -1.5, -2.0, -3.0, -4.0, -6.0])


def pack_weight(w, fmt):
    k, n = w.shape
    w = f64(np.asarray(w, np.float32).astype(ml_dtypes.bfloat16)).reshape(k // 32, 32, n)
    amax = np.abs(w).max(1)
    if fmt == "e4m3":
        byte = np.frexp(amax)[1] - 1 + 127 - 7
    else:
        mant, ex = np.frexp(amax / 6.0)
        byte = np.where(mant > 0.5, ex, ex - 1) + 127
    byte = np.clip(np.where(amax > 0, byte, 1), 1, 254)
    scaled = (w * np.exp2(127.0 - byte)[:, None, :]).reshape(k, n).astype(np.float32)
    by_word = np.ascontiguousarray(scaled.reshape(k // 512, 128, 4, n).transpose(0, 1, 3, 2))
    if fmt == "e4m3":
        words = by_word.astype(ml_dtypes.float8_e4m3fn).view(np.uint8)
    else:
        c = by_word.astype(ml_dtypes.float4_e2m1fn).view(np.uint8) & 0xF
        words = (c[..., 0::2] | (c[..., 1::2] << 4)).reshape(k // 512, 128, 2 * n)
    return np.ascontiguousarray(words), np.ascontiguousarray(byte.astype(np.uint8).reshape(k // 512, 16, n))


def unpack_weight(words, scales, fmt):
    g, _, n = scales.shape
    words = np.ascontiguousarray(words).reshape(g, 128, n, -1)
    if fmt == "e4m3":
        vals = words.view(ml_dtypes.float8_e4m3fn).astype(np.float64)
    else:
        nib = np.empty((g, 128, n, 4), np.uint8)
        nib[..., 0::2] = words & 0xF
        nib[..., 1::2] = words >> 4
        vals = E2M1[nib]
    vals = vals * np.repeat(np.exp2(scales.astype(np.float64) - 127.0), 8, axis=1)[..., None]
    return vals.transpose(0, 1, 3, 2).reshape(g * 512, n)


D, T, I, Q, E, U, X = 512, 2048, 512, 128, 512, 1024, 1024


def setup_inputs():
    n = np.random.standard_normal
    idx = np.random.permutation(T)[:I]
    idx2 = np.random.permutation(U)[:I]
    idx3 = np.random.permutation(X)[:I]
    fd = mx_kscale(D)
    fi = mx_kscale(I)
    keysp = pack_weight(n((D, T)) / fd[:, None], "e4m3")
    return {
        "query": (n((D, Q)) * 0.7 / np.sqrt(D) * fd[:, None]).astype(np.float32),
        "query2": (n((D, Q)) * 0.7 / np.sqrt(D) * fd[:, None]).astype(np.float32),
        "keys_words": keysp[0],
        "keys_scales": keysp[1],
        "notes": (n((D, U)) / fd[:, None]).astype(np.float32),
        "os": (np.random.uniform(0.02, 0.08, (1, I)) * fi).astype(np.float32),
        "vals": (n((E, T))).astype(np.float32),
        "vals2": (n((E, X))).astype(np.float32),
        "vsc": (np.random.uniform(0.5, 2.0, (1, I)) / fi).astype(np.float32),
        "offs": striped(idx),
        "offs2": striped(idx2),
        "offs3": striped(idx3),
    }


def reference(query, query2, keys_words, keys_scales, notes, os, vals, vals2, vsc, offs, offs2, offs3):
    idx = unstriped(offs)
    idx2 = unstriped(offs2)
    idx3 = unstriped(offs3)
    keysu = unpack_weight(keys_words, keys_scales, "e4m3")
    queryq = mxq(f64(query), 0, "e4m3")
    keysidxg = keysu[:, idx]
    query2q = mxq(f64(query2), 0, "e4m3")
    notesidx2q = mxq(f64(notes)[:, idx2], 0, "e4m3")
    w = queryq.T @ keysidxg + query2q.T @ notesidx2q
    wo1 = w * f64(os)
    wt1 = wo1.T
    vz = np.abs(f64(vals)[:, idx] - f64(vals2)[:, idx3]) * f64(vsc)
    vt1 = vz.T
    wt1q = mxq(wt1, 0, "e4m3")
    vt1q = mxq(vt1, 0, "e4m3")
    o = wt1q.T @ vt1q
    return o

@@ -1,0 +1,162 @@
+from contextlib import ExitStack
+
+import concourse.mybir as mybir
+from concourse.masks import make_identity
+
+D, T, I, Q, E, U, X = 512, 2048, 512, 128, 512, 1024, 1024
+FLOPS = 2 * Q * I * (2 * D + E)
+
+F32 = mybir.dt.float32
+BF16 = mybir.dt.bfloat16
+I32 = mybir.dt.int32
+U32 = mybir.dt.uint32
+U16 = mybir.dt.uint16
+U8 = mybir.dt.uint8
+FP8X4 = mybir.dt.float8_e4m3fn_x4
+ACT = mybir.ActivationFunctionType
+ALU = mybir.AluOpType
+
+P = 128
+PACK = 4
+BLOCKS = E // P
+
+
+def tile_attend_twosources_apartvalues_lean_kernel(
+    tc, query, query2, keys_words, keys_scales, notes, slot_os, vals, vals2, slot_vsc, offs, offs2, offs3, out
+):
+    nc = tc.nc
+    with ExitStack() as ctx:
+        sb = ctx.enter_context(tc.tile_pool(name="sb", bufs=1))
+        ps = ctx.enter_context(tc.psum_pool(name="ps", bufs=1))
+
+        idx = sb.tile([P, I // 16], U16, name="idx")
+        idx2 = sb.tile([P, I // 16], U16, name="idx2")
+        idx3 = sb.tile([P, I // 16], U16, name="idx3")
+        key_pool = sb.tile([P, T], U32, name="key_pool")
+        key_scale_pool = sb.tile([P, T], U8, name="key_scale_pool")
+        note_pool = [sb.tile([P, U], F32, name=f"note_pool{t}") for t in range(PACK)]
+        val_pool = [sb.tile([P, T], F32, name=f"val_pool{b}", tag=f"val{b}") for b in range(BLOCKS)]
+        val2_pool = [sb.tile([P, X], F32, name=f"val2_pool{b}") for b in range(BLOCKS)]
+        q_raw = [sb.tile([P, PACK, Q], F32, name=f"q_raw{a}") for a in range(2)]
+        os_col = sb.tile([P, 1, PACK], F32, name="os_col")
+        vsc_col = sb.tile([P, 1, PACK], F32, name="vsc_col")
+        ident = sb.tile([P, P], F32, name="ident")
+
+        nc.vector.memset(key_scale_pool[:].bitcast(I32), 0)
+        make_identity(nc, ident[:])
+
+        note_planes = notes.rearrange("(p t) u -> t p u", t=PACK)
+        nc.sync.dma_start(note_pool[0][:], note_planes[0])
+        nc.sync.dma_start(idx2[:], offs2)
+        nc.sync.dma_start(key_pool[:].bitcast(I32), keys_words[0].rearrange("p n t -> p (n t)").bitcast(I32))
+        nc.sync.dma_start(idx[:], offs)
+        for quad in range(4):
+            nc.sync.dma_start(
+                key_scale_pool[32 * quad : 32 * quad + 4, :].bitcast(I32),
+                keys_scales[0, 4 * quad : 4 * quad + 4, :].bitcast(I32),
+            )
+        for t in range(1, PACK):
+            nc.sync.dma_start(note_pool[t][:], note_planes[t])
+        for a, src in enumerate((query, query2)):
+            nc.sync.dma_start(q_raw[a][:], src.rearrange("(p t) q -> p t q", t=PACK))
+        nc.sync.dma_start(idx3[:], offs3)
+        nc.sync.dma_start(os_col[:], slot_os.rearrange("o (p t) -> p o t", t=PACK))
+        nc.sync.dma_start(vsc_col[:], slot_vsc.rearrange("o (p t) -> p o t", t=PACK))
+        for b in range(BLOCKS):
+            nc.sync.dma_start(val_pool[b][:], vals[P * b : P * (b + 1), :])
+            nc.sync.dma_start(val2_pool[b][:], vals2[P * b : P * (b + 1), :])
+
+        key_words = sb.tile([P, I], U32, name="key_words", align_bytes=64)
+        key_bytes = sb.tile([P, I], U8, name="key_bytes", align_bytes=64)
+        nc.vector.tensor_copy(key_words[:].rearrange("p (r s) -> p s r", r=PACK), key_pool[:].indirect(idx[:]))
+        nc.vector.tensor_copy(key_bytes[:].rearrange("p (r s) -> p s r", r=PACK), key_scale_pool[:].indirect(idx[:]))
+
+        note_g = sb.tile([P, PACK, I], BF16, name="note_g")
+        for t in range(PACK):
+            nc.scalar.activation(note_g[:, t, :], note_pool[t][:].indirect(idx2[:]), ACT.Copy)
+        note_woven = sb.tile([P, I * PACK], BF16, name="note_woven", tag="work2", align_bytes=64)
+        note_words = sb.tile([P, I], U32, name="note_words", align_bytes=64)
+        note_bytes = sb.tile([P, I], U8, name="note_bytes", align_bytes=64)
+
+        q_woven = sb.tile([P, 2, Q, PACK], BF16, name="q_woven", align_bytes=64)
+        q_words = sb.tile([P, 2 * Q], U32, name="q_words", align_bytes=64)
+        q_bytes = sb.tile([P, 2 * Q], U8, name="q_bytes", align_bytes=64)
+        for a in range(2):
+            nc.vector.tensor_copy(q_woven[:, a, :, :], q_raw[a][:].rearrange("p t q -> p q t"))
+        nc.vector.tensor_copy(
+            note_woven[:].rearrange("p (r s t) -> p r s t", r=PACK, t=PACK),
+            note_g[:].rearrange("p t (s r) -> p r s t", r=PACK),
+        )
+        nc.vector.quantize_mx(q_words[:].bitcast(FP8X4), q_bytes[:], q_woven[:].rearrange("p a q t -> p (a q t)"))
+        nc.vector.quantize_mx(note_words[:].bitcast(FP8X4), note_bytes[:], note_woven[:])
+
+        scores = ps.tile([P, PACK, Q], F32, name="scores")
+        for r in range(PACK):
+            cols = slice(P * r, P * (r + 1))
+            for a, (words, scale_bytes) in enumerate(((key_words, key_bytes), (note_words, note_bytes))):
+                q_cols = slice(Q * a, Q * (a + 1))
+                nc.tensor.matmul_mx(
+                    scores[:, r, :],
+                    lhsT=words[:, cols].bitcast(FP8X4),
+                    lhsT_scale=scale_bytes[:, cols],
+                    rhs=q_words[:, q_cols].bitcast(FP8X4),
+                    rhs_scale=q_bytes[:, q_cols],
+                    start=(a == 0),
+                    stop=(a == 1),
+                )
+        w_woven = sb.tile([P, Q, PACK], BF16, name="w_woven", align_bytes=64)
+        w_words = sb.tile([P, Q], U32, name="w_words", align_bytes=64)
+        w_bytes = sb.tile([P, Q], U8, name="w_bytes", align_bytes=64)
+        nc.vector.tensor_tensor(
+            w_woven[:], scores[:].rearrange("p r q -> p q r"), os_col[:].to_broadcast([P, Q, PACK]), ALU.mult
+        )
+        nc.vector.quantize_mx(w_words[:].bitcast(FP8X4), w_bytes[:], w_woven[:].rearrange("p q r -> p (q r)"))
+
+        def pick(b, tag):
+            picked = sb.tile([P, I], F32, name=f"picked{b}", tag=tag, align_bytes=64)
+            nc.scalar.activation(picked[:], val_pool[b][:].indirect(idx[:]), ACT.Copy)
+            return picked
+
+        def multiply(b, tag, turned, result):
+            v_woven = sb.tile([P, P, PACK], BF16, name=f"v_woven{b}", tag=tag, align_bytes=64)
+            v_words = sb.tile([P, P], U32, name=f"v_words{b}", align_bytes=64)
+            v_bytes = sb.tile([P, P], U8, name=f"v_bytes{b}", align_bytes=64)
+            nc.vector.tensor_tensor(
+                v_woven[:], turned[:].rearrange("p r e -> p e r"), vsc_col[:].to_broadcast([P, P, PACK]), ALU.mult
+            )
+            nc.vector.quantize_mx(v_words[:].bitcast(FP8X4), v_bytes[:], v_woven[:].rearrange("p e r -> p (e r)"))
+            nc.tensor.matmul_mx(
+                result,
+                lhsT=w_words[:].bitcast(FP8X4),
+                lhsT_scale=w_bytes[:],
+                rhs=v_words[:].bitcast(FP8X4),
+                rhs_scale=v_bytes[:],
+                start=True,
+                stop=True,
+            )
+
+        early_sums = ps.tile([P, BLOCKS - 1, P], F32, name="early_sums")
+        last_sums = ps.tile([P, P], F32, name="last_sums")
+        picked = [pick(0, "work0")]
+        turned = []
+        for b in range(BLOCKS):
+            diff = sb.tile([P, I], F32, name=f"diff{b}", tag=f"work{(b + 2) % 3}", align_bytes=64)
+            nc.vector.tensor_tensor(diff[:], val2_pool[b][:].indirect(idx3[:]), picked[b][:], ALU.subtract)
+            if b < BLOCKS - 1:
+                picked.append(pick(b + 1, f"work{(b + 1) % 3}"))
+            apart = sb.tile([P, PACK, P], F32, name=f"apart{b}", tag=f"val{b + 1}")
+            nc.scalar.activation(
+                apart[:].rearrange("p r s -> p s r"), diff[:].rearrange("p (s r) -> p s r", r=PACK), ACT.Abs
+            )
+            turned.append(ps.tile([P, PACK, P], F32, name=f"turned{b}"))
+            for r in range(PACK):
+                nc.tensor.transpose(turned[b][:, r, :], apart[:, r, :], ident[:])
+            if b > 0:
+                multiply(b - 1, f"work{b % 3}", turned[b - 1], early_sums[:, b - 1, :])
+        early = sb.tile([P, BLOCKS - 1, P], F32, name="early", tag=f"work{(BLOCKS + 1) % 3}", align_bytes=64)
+        last = sb.tile([P, P], F32, name="last")
+        nc.scalar.copy(early[:], early_sums[:])
+        nc.sync.dma_start(out[:, : (BLOCKS - 1) * P], early[:].rearrange("p b e -> p (b e)"))
+        multiply(BLOCKS - 1, f"work{BLOCKS % 3}", turned[BLOCKS - 1], last_sums[:])
+        nc.vector.tensor_copy(last[:], last_sums[:])
+        nc.sync.dma_start(out[:, (BLOCKS - 1) * P :], last[:])

@@ -35,8 +35,8 @@ def tile_attend_twosources_apartvalues_lean_kernel(
         key_pool = sb.tile([P, T], U32, name="key_pool")
         key_scale_pool = sb.tile([P, T], U8, name="key_scale_pool")
         note_pool = [sb.tile([P, U], F32, name=f"note_pool{t}") for t in range(PACK)]
-        val_pool = [sb.tile([P, T], F32, name=f"val_pool{b}", tag=f"val{b}") for b in range(BLOCKS)]
-        val2_pool = [sb.tile([P, X], F32, name=f"val2_pool{b}") for b in range(BLOCKS)]
+        val_pool = [sb.tile([P, T], F32, name=f"val_pool{b}") for b in range(BLOCKS)]
+        val2_pool = [sb.tile([P, X], F32, name=f"val2_pool{b}", tag=f"val2_{b}") for b in range(BLOCKS)]
         q_raw = [sb.tile([P, PACK, Q], F32, name=f"q_raw{a}") for a in range(2)]
         os_col = sb.tile([P, 1, PACK], F32, name="os_col")
         vsc_col = sb.tile([P, 1, PACK], F32, name="vsc_col")
@@ -50,12 +50,13 @@ def tile_attend_twosources_apartvalues_lean_kernel(
         nc.sync.dma_start(idx2[:], offs2)
         nc.sync.dma_start(key_pool[:].bitcast(I32), keys_words[0].rearrange("p n t -> p (n t)").bitcast(I32))
         nc.sync.dma_start(idx[:], offs)
-        for quad in range(4):
+        nc.sync.dma_start(note_pool[1][:], note_planes[1])
+        for row in range(4):
             nc.sync.dma_start(
-                key_scale_pool[32 * quad : 32 * quad + 4, :].bitcast(I32),
-                keys_scales[0, 4 * quad : 4 * quad + 4, :].bitcast(I32),
+                key_scale_pool[row:P:32, :].bitcast(I32),
+                keys_scales[0, row:16:4, :].bitcast(I32),
             )
-        for t in range(1, PACK):
+        for t in range(2, PACK):
             nc.sync.dma_start(note_pool[t][:], note_planes[t])
         for a, src in enumerate((query, query2)):
             nc.sync.dma_start(q_raw[a][:], src.rearrange("(p t) q -> p t q", t=PACK))
@@ -63,8 +64,8 @@ def tile_attend_twosources_apartvalues_lean_kernel(
         nc.sync.dma_start(os_col[:], slot_os.rearrange("o (p t) -> p o t", t=PACK))
         nc.sync.dma_start(vsc_col[:], slot_vsc.rearrange("o (p t) -> p o t", t=PACK))
         for b in range(BLOCKS):
-            nc.sync.dma_start(val_pool[b][:], vals[P * b : P * (b + 1), :])
             nc.sync.dma_start(val2_pool[b][:], vals2[P * b : P * (b + 1), :])
+            nc.sync.dma_start(val_pool[b][:], vals[P * b : P * (b + 1), :])
 
         key_words = sb.tile([P, I], U32, name="key_words", align_bytes=64)
         key_bytes = sb.tile([P, I], U8, name="key_bytes", align_bytes=64)
@@ -72,8 +73,9 @@ def tile_attend_twosources_apartvalues_lean_kernel(
         nc.vector.tensor_copy(key_bytes[:].rearrange("p (r s) -> p s r", r=PACK), key_scale_pool[:].indirect(idx[:]))
 
         note_g = sb.tile([P, PACK, I], BF16, name="note_g")
-        for t in range(PACK):
+        for t in range(PACK - 1):
             nc.scalar.activation(note_g[:, t, :], note_pool[t][:].indirect(idx2[:]), ACT.Copy)
+        nc.vector.tensor_copy(note_g[:, PACK - 1, :], note_pool[PACK - 1][:].indirect(idx2[:]))
         note_woven = sb.tile([P, I * PACK], BF16, name="note_woven", tag="work2", align_bytes=64)
         note_words = sb.tile([P, I], U32, name="note_words", align_bytes=64)
         note_bytes = sb.tile([P, I], U8, name="note_bytes", align_bytes=64)
@@ -84,8 +86,8 @@ def tile_attend_twosources_apartvalues_lean_kernel(
         for a in range(2):
             nc.vector.tensor_copy(q_woven[:, a, :, :], q_raw[a][:].rearrange("p t q -> p q t"))
         nc.vector.tensor_copy(
-            note_woven[:].rearrange("p (r s t) -> p r s t", r=PACK, t=PACK),
-            note_g[:].rearrange("p t (s r) -> p r s t", r=PACK),
+            note_woven[:].rearrange("p (r s t) -> p s r t", r=PACK, t=PACK),
+            note_g[:].rearrange("p t (s r) -> p s r t", r=PACK),
         )
         nc.vector.quantize_mx(q_words[:].bitcast(FP8X4), q_bytes[:], q_woven[:].rearrange("p a q t -> p (a q t)"))
         nc.vector.quantize_mx(note_words[:].bitcast(FP8X4), note_bytes[:], note_woven[:])
@@ -104,29 +106,30 @@ def tile_attend_twosources_apartvalues_lean_kernel(
                     start=(a == 0),
                     stop=(a == 1),
                 )
-        w_woven = sb.tile([P, Q, PACK], BF16, name="w_woven", align_bytes=64)
         w_words = sb.tile([P, Q], U32, name="w_words", align_bytes=64)
         w_bytes = sb.tile([P, Q], U8, name="w_bytes", align_bytes=64)
-        nc.vector.tensor_tensor(
-            w_woven[:], scores[:].rearrange("p r q -> p q r"), os_col[:].to_broadcast([P, Q, PACK]), ALU.mult
-        )
-        nc.vector.quantize_mx(w_words[:].bitcast(FP8X4), w_bytes[:], w_woven[:].rearrange("p q r -> p (q r)"))
 
-        def pick(b, tag):
-            picked = sb.tile([P, I], F32, name=f"picked{b}", tag=tag, align_bytes=64)
-            nc.scalar.activation(picked[:], val_pool[b][:].indirect(idx[:]), ACT.Copy)
-            return picked
+        def scale_and_quantize(name, tag, bank, factor, words, scale_bytes):
+            woven = sb.tile([P, P, PACK], BF16, name=name, tag=tag, align_bytes=64)
+            halves = [slice(P // 2 * h, P // 2 * (h + 1)) for h in range(2)]
+            for cols in halves:
+                nc.vector.tensor_tensor(
+                    woven[:, cols, :],
+                    bank[:, :, cols].rearrange("p r c -> p c r"),
+                    factor[:].to_broadcast([P, P // 2, PACK]),
+                    ALU.mult,
+                )
+            for cols in halves:
+                nc.vector.quantize_mx(
+                    words[:, cols].bitcast(FP8X4), scale_bytes[:, cols], woven[:, cols, :].rearrange("p c r -> p (c r)")
+                )
 
-        def multiply(b, tag, turned, result):
-            v_woven = sb.tile([P, P, PACK], BF16, name=f"v_woven{b}", tag=tag, align_bytes=64)
+        def multiply(b, turned, sums):
             v_words = sb.tile([P, P], U32, name=f"v_words{b}", align_bytes=64)
             v_bytes = sb.tile([P, P], U8, name=f"v_bytes{b}", align_bytes=64)
-            nc.vector.tensor_tensor(
-                v_woven[:], turned[:].rearrange("p r e -> p e r"), vsc_col[:].to_broadcast([P, P, PACK]), ALU.mult
-            )
-            nc.vector.quantize_mx(v_words[:].bitcast(FP8X4), v_bytes[:], v_woven[:].rearrange("p e r -> p (e r)"))
+            scale_and_quantize(f"v_woven{b}", f"work{(b + 1) % 3 if b < BLOCKS - 1 else 2}", turned, vsc_col, v_words, v_bytes)
             nc.tensor.matmul_mx(
-                result,
+                sums,
                 lhsT=w_words[:].bitcast(FP8X4),
                 lhsT_scale=w_bytes[:],
                 rhs=v_words[:].bitcast(FP8X4),
@@ -137,26 +140,50 @@ def tile_attend_twosources_apartvalues_lean_kernel(
 
         early_sums = ps.tile([P, BLOCKS - 1, P], F32, name="early_sums")
         last_sums = ps.tile([P, P], F32, name="last_sums")
-        picked = [pick(0, "work0")]
+        half = I // 2
+
+        def pick2(b):
+            picked = sb.tile([P, I], F32, name=f"picked2_{b}", tag=f"work{b % 3}", align_bytes=64)
+            nc.scalar.activation(picked[:], val2_pool[b][:].indirect(idx3[:]), ACT.Copy)
+            return picked
+
+        def deal_abs(apart, signed):
+            nc.scalar.activation(
+                apart.rearrange("p r s -> p s r"), signed.rearrange("p (s r) -> p s r", r=PACK), ACT.Abs
+            )
+
+        picked2 = [pick2(0)]
         turned = []
         for b in range(BLOCKS):
-            diff = sb.tile([P, I], F32, name=f"diff{b}", tag=f"work{(b + 2) % 3}", align_bytes=64)
-            nc.vector.tensor_tensor(diff[:], val2_pool[b][:].indirect(idx3[:]), picked[b][:], ALU.subtract)
+            apart_tag = f"val2_{b + 1}"
             if b < BLOCKS - 1:
-                picked.append(pick(b + 1, f"work{(b + 1) % 3}"))
-            apart = sb.tile([P, PACK, P], F32, name=f"apart{b}", tag=f"val{b + 1}")
-            nc.scalar.activation(
-                apart[:].rearrange("p r s -> p s r"), diff[:].rearrange("p (s r) -> p s r", r=PACK), ACT.Abs
-            )
+                diff = sb.tile([P, I], F32, name=f"diff{b}", tag=f"work{(b + 2) % 3}", align_bytes=64)
+                nc.vector.tensor_tensor(diff[:], val_pool[b][:].indirect(idx[:]), picked2[b][:], ALU.subtract)
+                picked2.append(pick2(b + 1))
+                apart = sb.tile([P, PACK, P], F32, name=f"apart{b}", tag=apart_tag)
+                deal_abs(apart[:], diff[:])
+            else:
+                diff = sb.tile([P, half], F32, name=f"diff{b}", tag=f"work{(b + 2) % 3}", align_bytes=64)
+                other = sb.tile([P, half], F32, name="other", tag=f"work{(b + 1) % 3}", align_bytes=64)
+                nc.vector.tensor_tensor(
+                    diff[:], val_pool[b][:].indirect(idx[:, : half // 16]), picked2[b][:, :half], ALU.subtract
+                )
+                nc.scalar.activation(other[:], val_pool[b][:].indirect(idx[:, half // 16 :]), ACT.Copy)
+                nc.vector.tensor_tensor(other[:], other[:], picked2[b][:, half:], ALU.subtract)
+                apart = sb.tile([P, PACK, P], F32, name=f"apart{b}", tag=apart_tag)
+                deal_abs(apart[:, :, : P // 2], diff[:])
+                deal_abs(apart[:, :, P // 2 :], other[:])
             turned.append(ps.tile([P, PACK, P], F32, name=f"turned{b}"))
             for r in range(PACK):
                 nc.tensor.transpose(turned[b][:, r, :], apart[:, r, :], ident[:])
-            if b > 0:
-                multiply(b - 1, f"work{b % 3}", turned[b - 1], early_sums[:, b - 1, :])
-        early = sb.tile([P, BLOCKS - 1, P], F32, name="early", tag=f"work{(BLOCKS + 1) % 3}", align_bytes=64)
+            if b == 0:
+                scale_and_quantize("w_woven", "work0", scores, os_col, w_words, w_bytes)
+            else:
+                multiply(b - 1, turned[b - 1], early_sums[:, b - 1, :])
+        early = sb.tile([P, BLOCKS - 1, P], F32, name="early", tag="work1", align_bytes=64)
         last = sb.tile([P, P], F32, name="last")
         nc.scalar.copy(early[:], early_sums[:])
         nc.sync.dma_start(out[:, : (BLOCKS - 1) * P], early[:].rearrange("p b e -> p (b e)"))
-        multiply(BLOCKS - 1, f"work{BLOCKS % 3}", turned[BLOCKS - 1], last_sums[:])
-        nc.vector.tensor_copy(last[:], last_sums[:])
-        nc.sync.dma_start(out[:, (BLOCKS - 1) * P :], last[:])
+        multiply(BLOCKS - 1, turned[BLOCKS - 1], last_sums[:])
+        nc.scalar.copy(last[:], last_sums[:])
+        nc.scalar.dma_start(out[:, (BLOCKS - 1) * P :], last[:])

@@ -34,48 +34,53 @@ def tile_attend_twosources_apartvalues_lean_kernel(
         idx3 = sb.tile([P, I // 16], U16, name="idx3")
         key_pool = sb.tile([P, T], U32, name="key_pool")
         key_scale_pool = sb.tile([P, T], U8, name="key_scale_pool")
-        note_pool = [sb.tile([P, U], F32, name=f"note_pool{t}") for t in range(PACK)]
+        note_pool = [sb.tile([P, 2, U], F32, name=f"note_pool{h}") for h in range(2)]
         val_pool = [sb.tile([P, T], F32, name=f"val_pool{b}") for b in range(BLOCKS)]
         val2_pool = [sb.tile([P, X], F32, name=f"val2_pool{b}", tag=f"val2_{b}") for b in range(BLOCKS)]
         q_raw = [sb.tile([P, PACK, Q], F32, name=f"q_raw{a}") for a in range(2)]
-        os_col = sb.tile([P, 1, PACK], F32, name="os_col")
-        vsc_col = sb.tile([P, 1, PACK], F32, name="vsc_col")
+        factor_rows = sb.tile([P, I], F32, name="factor_rows")
+        factors = sb.tile([P, 2, PACK], F32, name="factors")
         ident = sb.tile([P, P], F32, name="ident")
 
         nc.vector.memset(key_scale_pool[:].bitcast(I32), 0)
+        nc.vector.memset(factor_rows[:], 0.0)
         make_identity(nc, ident[:])
 
-        note_planes = notes.rearrange("(p t) u -> t p u", t=PACK)
+        note_planes = notes.rearrange("(p h j) u -> h p j u", h=2, j=2)
         nc.sync.dma_start(note_pool[0][:], note_planes[0])
         nc.sync.dma_start(idx2[:], offs2)
         nc.sync.dma_start(key_pool[:].bitcast(I32), keys_words[0].rearrange("p n t -> p (n t)").bitcast(I32))
         nc.sync.dma_start(idx[:], offs)
-        nc.sync.dma_start(note_pool[1][:], note_planes[1])
         for row in range(4):
             nc.sync.dma_start(
                 key_scale_pool[row:P:32, :].bitcast(I32),
                 keys_scales[0, row:16:4, :].bitcast(I32),
             )
-        for t in range(2, PACK):
-            nc.sync.dma_start(note_pool[t][:], note_planes[t])
+        nc.sync.dma_start(note_pool[1][:], note_planes[1])
+        nc.sync.dma_start(factor_rows[0:1, :], slot_os)
+        nc.sync.dma_start(factor_rows[1:2, :], slot_vsc)
         for a, src in enumerate((query, query2)):
             nc.sync.dma_start(q_raw[a][:], src.rearrange("(p t) q -> p t q", t=PACK))
         nc.sync.dma_start(idx3[:], offs3)
-        nc.sync.dma_start(os_col[:], slot_os.rearrange("o (p t) -> p o t", t=PACK))
-        nc.sync.dma_start(vsc_col[:], slot_vsc.rearrange("o (p t) -> p o t", t=PACK))
         for b in range(BLOCKS):
             nc.sync.dma_start(val2_pool[b][:], vals2[P * b : P * (b + 1), :])
             nc.sync.dma_start(val_pool[b][:], vals[P * b : P * (b + 1), :])
+
+        factors_turned = ps.tile([P, PACK, P], F32, name="factors_turned")
+        for r in range(PACK):
+            nc.tensor.transpose(factors_turned[:, r, :], factor_rows[:, r:I:PACK], ident[:])
+        nc.vector.tensor_copy(factors[:], factors_turned[:, :, 0:2].rearrange("p r a -> p a r"))
+        os_col, vsc_col = factors[:, 0:1, :], factors[:, 1:2, :]
 
         key_words = sb.tile([P, I], U32, name="key_words", align_bytes=64)
         key_bytes = sb.tile([P, I], U8, name="key_bytes", align_bytes=64)
         nc.vector.tensor_copy(key_words[:].rearrange("p (r s) -> p s r", r=PACK), key_pool[:].indirect(idx[:]))
         nc.vector.tensor_copy(key_bytes[:].rearrange("p (r s) -> p s r", r=PACK), key_scale_pool[:].indirect(idx[:]))
 
-        note_g = sb.tile([P, PACK, I], BF16, name="note_g")
+        note_g = sb.tile([P, PACK, I], F32, name="note_g")
         for t in range(PACK - 1):
-            nc.scalar.activation(note_g[:, t, :], note_pool[t][:].indirect(idx2[:]), ACT.Copy)
-        nc.vector.tensor_copy(note_g[:, PACK - 1, :], note_pool[PACK - 1][:].indirect(idx2[:]))
+            nc.scalar.activation(note_g[:, t, :], note_pool[t // 2][:, t % 2, :].indirect(idx2[:]), ACT.Copy)
+        nc.vector.tensor_copy(note_g[:, PACK - 1, :], note_pool[1][:, 1, :].indirect(idx2[:]))
         note_woven = sb.tile([P, I * PACK], BF16, name="note_woven", tag="work2", align_bytes=64)
         note_words = sb.tile([P, I], U32, name="note_words", align_bytes=64)
         note_bytes = sb.tile([P, I], U8, name="note_bytes", align_bytes=64)
@@ -116,7 +121,7 @@ def tile_attend_twosources_apartvalues_lean_kernel(
                 nc.vector.tensor_tensor(
                     woven[:, cols, :],
                     bank[:, :, cols].rearrange("p r c -> p c r"),
-                    factor[:].to_broadcast([P, P // 2, PACK]),
+                    factor.to_broadcast([P, P // 2, PACK]),
                     ALU.mult,
                 )
             for cols in halves:

@@ -35,7 +35,7 @@ def tile_attend_twosources_apartvalues_lean_kernel(
         key_pool = sb.tile([P, T], U32, name="key_pool")
         key_scale_pool = sb.tile([P, T], U8, name="key_scale_pool")
         note_pool = [sb.tile([P, 2, U], F32, name=f"note_pool{h}") for h in range(2)]
-        val_pool = [sb.tile([P, T], F32, name=f"val_pool{b}") for b in range(BLOCKS)]
+        val_pool = [sb.tile([P, T], F32, name=f"val_pool{b}", tag=f"val_{b}", align_bytes=64) for b in range(BLOCKS)]
         val2_pool = [sb.tile([P, X], F32, name=f"val2_pool{b}", tag=f"val2_{b}") for b in range(BLOCKS)]
         q_raw = [sb.tile([P, PACK, Q], F32, name=f"q_raw{a}") for a in range(2)]
         factor_rows = sb.tile([P, I], F32, name="factor_rows")
@@ -47,10 +47,12 @@ def tile_attend_twosources_apartvalues_lean_kernel(
         make_identity(nc, ident[:])
 
         note_planes = notes.rearrange("(p h j) u -> h p j u", h=2, j=2)
-        nc.sync.dma_start(note_pool[0][:], note_planes[0])
-        nc.sync.dma_start(idx2[:], offs2)
+        for a, src in enumerate((query, query2)):
+            nc.sync.dma_start(q_raw[a][:], src.rearrange("(p t) q -> p t q", t=PACK))
         nc.sync.dma_start(key_pool[:].bitcast(I32), keys_words[0].rearrange("p n t -> p (n t)").bitcast(I32))
         nc.sync.dma_start(idx[:], offs)
+        nc.sync.dma_start(note_pool[0][:], note_planes[0])
+        nc.sync.dma_start(idx2[:], offs2)
         for row in range(4):
             nc.sync.dma_start(
                 key_scale_pool[row:P:32, :].bitcast(I32),
@@ -59,8 +61,6 @@ def tile_attend_twosources_apartvalues_lean_kernel(
         nc.sync.dma_start(note_pool[1][:], note_planes[1])
         nc.sync.dma_start(factor_rows[0:1, :], slot_os)
         nc.sync.dma_start(factor_rows[1:2, :], slot_vsc)
-        for a, src in enumerate((query, query2)):
-            nc.sync.dma_start(q_raw[a][:], src.rearrange("(p t) q -> p t q", t=PACK))
         nc.sync.dma_start(idx3[:], offs3)
         for b in range(BLOCKS):
             nc.sync.dma_start(val2_pool[b][:], vals2[P * b : P * (b + 1), :])
@@ -77,24 +77,25 @@ def tile_attend_twosources_apartvalues_lean_kernel(
         nc.vector.tensor_copy(key_words[:].rearrange("p (r s) -> p s r", r=PACK), key_pool[:].indirect(idx[:]))
         nc.vector.tensor_copy(key_bytes[:].rearrange("p (r s) -> p s r", r=PACK), key_scale_pool[:].indirect(idx[:]))
 
-        note_g = sb.tile([P, PACK, I], F32, name="note_g")
-        for t in range(PACK - 1):
-            nc.scalar.activation(note_g[:, t, :], note_pool[t // 2][:, t % 2, :].indirect(idx2[:]), ACT.Copy)
-        nc.vector.tensor_copy(note_g[:, PACK - 1, :], note_pool[1][:, 1, :].indirect(idx2[:]))
-        note_woven = sb.tile([P, I * PACK], BF16, name="note_woven", tag="work2", align_bytes=64)
-        note_words = sb.tile([P, I], U32, name="note_words", align_bytes=64)
-        note_bytes = sb.tile([P, I], U8, name="note_bytes", align_bytes=64)
-
         q_woven = sb.tile([P, 2, Q, PACK], BF16, name="q_woven", align_bytes=64)
         q_words = sb.tile([P, 2 * Q], U32, name="q_words", align_bytes=64)
         q_bytes = sb.tile([P, 2 * Q], U8, name="q_bytes", align_bytes=64)
         for a in range(2):
-            nc.vector.tensor_copy(q_woven[:, a, :, :], q_raw[a][:].rearrange("p t q -> p q t"))
+            nc.scalar.activation(q_woven[:, a, :, :], q_raw[a][:].rearrange("p t q -> p q t"), ACT.Copy)
+        nc.vector.quantize_mx(q_words[:].bitcast(FP8X4), q_bytes[:], q_woven[:].rearrange("p a q t -> p (a q t)"))
+
+        note_g = sb.tile([P, PACK, I], F32, name="note_g")
+        for t in range(PACK - 1):
+            nc.scalar.activation(note_g[:, t, :], note_pool[t // 2][:, t % 2, :].indirect(idx2[:]), ACT.Copy)
+        nc.vector.tensor_copy(note_g[:, PACK - 1, :], note_pool[1][:, 1, :].indirect(idx2[:]))
+        note_woven = sb.tile([P, I * PACK], BF16, name="note_woven", tag="val_-1", align_bytes=64)
+        note_words = sb.tile([P, I], U32, name="note_words", align_bytes=64)
+        note_bytes = sb.tile([P, I], U8, name="note_bytes", align_bytes=64)
+
         nc.vector.tensor_copy(
             note_woven[:].rearrange("p (r s t) -> p s r t", r=PACK, t=PACK),
             note_g[:].rearrange("p t (s r) -> p s r t", r=PACK),
         )
-        nc.vector.quantize_mx(q_words[:].bitcast(FP8X4), q_bytes[:], q_woven[:].rearrange("p a q t -> p (a q t)"))
         nc.vector.quantize_mx(note_words[:].bitcast(FP8X4), note_bytes[:], note_woven[:])
 
         scores = ps.tile([P, PACK, Q], F32, name="scores")
@@ -114,25 +115,23 @@ def tile_attend_twosources_apartvalues_lean_kernel(
         w_words = sb.tile([P, Q], U32, name="w_words", align_bytes=64)
         w_bytes = sb.tile([P, Q], U8, name="w_bytes", align_bytes=64)
 
-        def scale_and_quantize(name, tag, bank, factor, words, scale_bytes):
+        halves = [slice(P // 2 * h, P // 2 * (h + 1)) for h in range(2)]
+
+        def scale_and_quantize(name, tag, source, factor, words, scale_bytes):
             woven = sb.tile([P, P, PACK], BF16, name=name, tag=tag, align_bytes=64)
-            halves = [slice(P // 2 * h, P // 2 * (h + 1)) for h in range(2)]
             for cols in halves:
                 nc.vector.tensor_tensor(
-                    woven[:, cols, :],
-                    bank[:, :, cols].rearrange("p r c -> p c r"),
-                    factor.to_broadcast([P, P // 2, PACK]),
-                    ALU.mult,
+                    woven[:, cols, :], source[:, cols, :], factor.to_broadcast([P, P // 2, PACK]), ALU.mult
                 )
             for cols in halves:
                 nc.vector.quantize_mx(
                     words[:, cols].bitcast(FP8X4), scale_bytes[:, cols], woven[:, cols, :].rearrange("p c r -> p (c r)")
                 )
 
-        def multiply(b, turned, sums):
+        def multiply(b, apart, sums):
             v_words = sb.tile([P, P], U32, name=f"v_words{b}", align_bytes=64)
             v_bytes = sb.tile([P, P], U8, name=f"v_bytes{b}", align_bytes=64)
-            scale_and_quantize(f"v_woven{b}", f"work{(b + 1) % 3 if b < BLOCKS - 1 else 2}", turned, vsc_col, v_words, v_bytes)
+            scale_and_quantize(f"v_woven{b}", f"val_{b + 1}", apart[:], vsc_col, v_words, v_bytes)
             nc.tensor.matmul_mx(
                 sums,
                 lhsT=w_words[:].bitcast(FP8X4),
@@ -143,52 +142,55 @@ def tile_attend_twosources_apartvalues_lean_kernel(
                 stop=True,
             )
 
-        early_sums = ps.tile([P, BLOCKS - 1, P], F32, name="early_sums")
-        last_sums = ps.tile([P, P], F32, name="last_sums")
-        half = I // 2
-
         def pick2(b):
-            picked = sb.tile([P, I], F32, name=f"picked2_{b}", tag=f"work{b % 3}", align_bytes=64)
-            nc.scalar.activation(picked[:], val2_pool[b][:].indirect(idx3[:]), ACT.Copy)
-            return picked
+            tag = f"val_{b - 3}" if b >= 2 else f"negated{b}"
+            negated = sb.tile([P, I], F32, name=f"negated{b}", tag=tag, align_bytes=64)
+            nc.scalar.activation(negated[:], val2_pool[b][:].indirect(idx3[:]), ACT.Copy, scale=-1.0)
+            return negated
 
-        def deal_abs(apart, signed):
-            nc.scalar.activation(
-                apart.rearrange("p r s -> p s r"), signed.rearrange("p (s r) -> p s r", r=PACK), ACT.Abs
-            )
-
-        picked2 = [pick2(0)]
-        turned = []
-        for b in range(BLOCKS):
-            apart_tag = f"val2_{b + 1}"
-            if b < BLOCKS - 1:
-                diff = sb.tile([P, I], F32, name=f"diff{b}", tag=f"work{(b + 2) % 3}", align_bytes=64)
-                nc.vector.tensor_tensor(diff[:], val_pool[b][:].indirect(idx[:]), picked2[b][:], ALU.subtract)
-                picked2.append(pick2(b + 1))
-                apart = sb.tile([P, PACK, P], F32, name=f"apart{b}", tag=apart_tag)
-                deal_abs(apart[:], diff[:])
-            else:
-                diff = sb.tile([P, half], F32, name=f"diff{b}", tag=f"work{(b + 2) % 3}", align_bytes=64)
-                other = sb.tile([P, half], F32, name="other", tag=f"work{(b + 1) % 3}", align_bytes=64)
-                nc.vector.tensor_tensor(
-                    diff[:], val_pool[b][:].indirect(idx[:, : half // 16]), picked2[b][:, :half], ALU.subtract
-                )
-                nc.scalar.activation(other[:], val_pool[b][:].indirect(idx[:, half // 16 :]), ACT.Copy)
-                nc.vector.tensor_tensor(other[:], other[:], picked2[b][:, half:], ALU.subtract)
-                apart = sb.tile([P, PACK, P], F32, name=f"apart{b}", tag=apart_tag)
-                deal_abs(apart[:, :, : P // 2], diff[:])
-                deal_abs(apart[:, :, P // 2 :], other[:])
-            turned.append(ps.tile([P, PACK, P], F32, name=f"turned{b}"))
+        def turn(bank, source, first):
             for r in range(PACK):
-                nc.tensor.transpose(turned[b][:, r, :], apart[:, r, :], ident[:])
-            if b == 0:
-                scale_and_quantize("w_woven", "work0", scores, os_col, w_words, w_bytes)
+                nc.tensor.matmul(
+                    bank[:, r, :],
+                    lhsT=source[:, r:I:PACK],
+                    rhs=ident[:],
+                    is_transpose=True,
+                    start=(first and r == 0),
+                    stop=(not first and r == PACK - 1),
+                )
+
+        early_sums = ps.tile([P, 2, P], F32, name="early_sums")
+        late_sums = [ps.tile([P, P], F32, name=f"late_sums{j}") for j in range(2)]
+        half = I // 2
+        negated = pick2(0)
+        apart = []
+        for b in range(BLOCKS):
+            turned = ps.tile([P, PACK, P], F32, name=f"turned{b}", tag=f"turned{b % 2}")
+            turn(turned, negated, True)
+            picked = sb.tile([P, I], F32, name=f"picked{b}", tag=f"val_{b - 1}", align_bytes=64)
+            if b < BLOCKS - 1:
+                nc.vector.tensor_copy(picked[:], val_pool[b][:].indirect(idx[:]))
             else:
-                multiply(b - 1, turned[b - 1], early_sums[:, b - 1, :])
-        early = sb.tile([P, BLOCKS - 1, P], F32, name="early", tag="work1", align_bytes=64)
+                nc.vector.tensor_copy(picked[:, :half], val_pool[b][:].indirect(idx[:, : half // 16]))
+                nc.scalar.activation(picked[:, half:], val_pool[b][:].indirect(idx[:, half // 16 :]), ACT.Copy)
+            turn(turned, picked, False)
+            if b < BLOCKS - 1:
+                negated = pick2(b + 1)
+            apart.append(sb.tile([P, P, PACK], F32, name=f"apart{b}", tag=f"val2_{b + 1}"))
+            for cols in halves if b == BLOCKS - 1 else [slice(0, P)]:
+                nc.scalar.activation(apart[b][:, cols, :], turned[:, :, cols].rearrange("p r e -> p e r"), ACT.Abs)
+            if b == 0:
+                scale_and_quantize("w_woven", "val_0", scores[:].rearrange("p r q -> p q r"), os_col, w_words, w_bytes)
+            else:
+                multiply(b - 1, apart[b - 1], early_sums[:, b - 1, :] if b < BLOCKS - 1 else late_sums[0][:])
+            if b == BLOCKS - 2:
+                early = sb.tile([P, 2, P], F32, name="early")
+                nc.vector.tensor_copy(early[:], early_sums[:])
+                nc.sync.dma_start(out[:, : 2 * P], early[:].rearrange("p b e -> p (b e)"))
+        multiply(BLOCKS - 1, apart[BLOCKS - 1], late_sums[1][:])
+        third = sb.tile([P, P], F32, name="third", tag=f"val2_{BLOCKS}")
+        nc.scalar.copy(third[:], late_sums[0][:])
+        nc.sync.dma_start(out[:, 2 * P : 3 * P], third[:])
         last = sb.tile([P, P], F32, name="last")
-        nc.scalar.copy(early[:], early_sums[:])
-        nc.sync.dma_start(out[:, : (BLOCKS - 1) * P], early[:].rearrange("p b e -> p (b e)"))
-        multiply(BLOCKS - 1, turned[BLOCKS - 1], last_sums[:])
-        nc.scalar.copy(last[:], last_sums[:])
-        nc.scalar.dma_start(out[:, (BLOCKS - 1) * P :], last[:])
+        nc.scalar.copy(last[:], late_sums[1][:])
+        nc.scalar.dma_start(out[:, 3 * P :], last[:])

from contextlib import ExitStack

import concourse.mybir as mybir
from concourse.masks import make_identity

D, T, I, Q, E, U, X = 512, 2048, 512, 128, 512, 1024, 1024
FLOPS = 2 * Q * I * (2 * D + E)

F32 = mybir.dt.float32
BF16 = mybir.dt.bfloat16
I32 = mybir.dt.int32
U32 = mybir.dt.uint32
U16 = mybir.dt.uint16
U8 = mybir.dt.uint8
FP8X4 = mybir.dt.float8_e4m3fn_x4
ACT = mybir.ActivationFunctionType
ALU = mybir.AluOpType

P = 128
PACK = 4
BLOCKS = E // P


def tile_attend_twosources_apartvalues_lean_kernel(
    tc, query, query2, keys_words, keys_scales, notes, slot_os, vals, vals2, slot_vsc, offs, offs2, offs3, out
):
    nc = tc.nc
    with ExitStack() as ctx:
        sb = ctx.enter_context(tc.tile_pool(name="sb", bufs=1))
        ps = ctx.enter_context(tc.psum_pool(name="ps", bufs=1))

        idx = sb.tile([P, I // 16], U16, name="idx")
        idx2 = sb.tile([P, I // 16], U16, name="idx2")
        idx3 = sb.tile([P, I // 16], U16, name="idx3")
        key_pool = sb.tile([P, T], U32, name="key_pool")
        key_scale_pool = sb.tile([P, T], U8, name="key_scale_pool")
        note_pool = [sb.tile([P, 2, U], F32, name=f"note_pool{h}") for h in range(2)]
        val_pool = [sb.tile([P, T], F32, name=f"val_pool{b}", tag=f"val_{b}", align_bytes=64) for b in range(BLOCKS)]
        val2_pool = [sb.tile([P, X], F32, name=f"val2_pool{b}", tag=f"val2_{b}") for b in range(BLOCKS)]
        q_raw = [sb.tile([P, PACK, Q], F32, name=f"q_raw{a}") for a in range(2)]
        factor_rows = sb.tile([P, I], F32, name="factor_rows")
        factors = sb.tile([P, 2, PACK], F32, name="factors")
        ident = sb.tile([P, P], F32, name="ident")

        nc.vector.memset(key_scale_pool[:].bitcast(I32), 0)
        nc.vector.memset(factor_rows[:], 0.0)
        make_identity(nc, ident[:])

        note_planes = notes.rearrange("(p h j) u -> h p j u", h=2, j=2)
        for a, src in enumerate((query, query2)):
            nc.sync.dma_start(q_raw[a][:], src.rearrange("(p t) q -> p t q", t=PACK))
        nc.sync.dma_start(key_pool[:].bitcast(I32), keys_words[0].rearrange("p n t -> p (n t)").bitcast(I32))
        nc.sync.dma_start(idx[:], offs)
        nc.sync.dma_start(note_pool[0][:], note_planes[0])
        nc.sync.dma_start(idx2[:], offs2)
        for row in range(4):
            nc.sync.dma_start(
                key_scale_pool[row:P:32, :].bitcast(I32),
                keys_scales[0, row:16:4, :].bitcast(I32),
            )
        nc.sync.dma_start(note_pool[1][:], note_planes[1])
        nc.sync.dma_start(factor_rows[0:1, :], slot_os)
        nc.sync.dma_start(factor_rows[1:2, :], slot_vsc)
        nc.sync.dma_start(idx3[:], offs3)
        for b in range(BLOCKS):
            nc.sync.dma_start(val2_pool[b][:], vals2[P * b : P * (b + 1), :])
            nc.sync.dma_start(val_pool[b][:], vals[P * b : P * (b + 1), :])

        factors_turned = ps.tile([P, PACK, P], F32, name="factors_turned")
        for r in range(PACK):
            nc.tensor.transpose(factors_turned[:, r, :], factor_rows[:, r:I:PACK], ident[:])
        nc.vector.tensor_copy(factors[:], factors_turned[:, :, 0:2].rearrange("p r a -> p a r"))
        os_col, vsc_col = factors[:, 0:1, :], factors[:, 1:2, :]

        key_words = sb.tile([P, I], U32, name="key_words", align_bytes=64)
        key_bytes = sb.tile([P, I], U8, name="key_bytes", align_bytes=64)
        nc.vector.tensor_copy(key_words[:].rearrange("p (r s) -> p s r", r=PACK), key_pool[:].indirect(idx[:]))
        nc.vector.tensor_copy(key_bytes[:].rearrange("p (r s) -> p s r", r=PACK), key_scale_pool[:].indirect(idx[:]))

        q_woven = sb.tile([P, 2, Q, PACK], BF16, name="q_woven", align_bytes=64)
        q_words = sb.tile([P, 2 * Q], U32, name="q_words", align_bytes=64)
        q_bytes = sb.tile([P, 2 * Q], U8, name="q_bytes", align_bytes=64)
        for a in range(2):
            nc.scalar.activation(q_woven[:, a, :, :], q_raw[a][:].rearrange("p t q -> p q t"), ACT.Copy)
        nc.vector.quantize_mx(q_words[:].bitcast(FP8X4), q_bytes[:], q_woven[:].rearrange("p a q t -> p (a q t)"))

        note_g = sb.tile([P, PACK, I], F32, name="note_g")
        for t in range(PACK - 1):
            nc.scalar.activation(note_g[:, t, :], note_pool[t // 2][:, t % 2, :].indirect(idx2[:]), ACT.Copy)
        nc.vector.tensor_copy(note_g[:, PACK - 1, :], note_pool[1][:, 1, :].indirect(idx2[:]))
        note_woven = sb.tile([P, I * PACK], BF16, name="note_woven", tag="val_-1", align_bytes=64)
        note_words = sb.tile([P, I], U32, name="note_words", align_bytes=64)
        note_bytes = sb.tile([P, I], U8, name="note_bytes", align_bytes=64)

        nc.vector.tensor_copy(
            note_woven[:].rearrange("p (r s t) -> p s r t", r=PACK, t=PACK),
            note_g[:].rearrange("p t (s r) -> p s r t", r=PACK),
        )
        nc.vector.quantize_mx(note_words[:].bitcast(FP8X4), note_bytes[:], note_woven[:])

        scores = ps.tile([P, PACK, Q], F32, name="scores")
        for r in range(PACK):
            cols = slice(P * r, P * (r + 1))
            for a, (words, scale_bytes) in enumerate(((key_words, key_bytes), (note_words, note_bytes))):
                q_cols = slice(Q * a, Q * (a + 1))
                nc.tensor.matmul_mx(
                    scores[:, r, :],
                    lhsT=words[:, cols].bitcast(FP8X4),
                    lhsT_scale=scale_bytes[:, cols],
                    rhs=q_words[:, q_cols].bitcast(FP8X4),
                    rhs_scale=q_bytes[:, q_cols],
                    start=(a == 0),
                    stop=(a == 1),
                )
        w_words = sb.tile([P, Q], U32, name="w_words", align_bytes=64)
        w_bytes = sb.tile([P, Q], U8, name="w_bytes", align_bytes=64)

        halves = [slice(P // 2 * h, P // 2 * (h + 1)) for h in range(2)]

        def scale_and_quantize(name, tag, source, factor, words, scale_bytes):
            woven = sb.tile([P, P, PACK], BF16, name=name, tag=tag, align_bytes=64)
            for cols in halves:
                nc.vector.tensor_tensor(
                    woven[:, cols, :], source[:, cols, :], factor.to_broadcast([P, P // 2, PACK]), ALU.mult
                )
            for cols in halves:
                nc.vector.quantize_mx(
                    words[:, cols].bitcast(FP8X4), scale_bytes[:, cols], woven[:, cols, :].rearrange("p c r -> p (c r)")
                )

        def multiply(b, apart, sums):
            v_words = sb.tile([P, P], U32, name=f"v_words{b}", align_bytes=64)
            v_bytes = sb.tile([P, P], U8, name=f"v_bytes{b}", align_bytes=64)
            scale_and_quantize(f"v_woven{b}", f"val_{b + 1}", apart[:], vsc_col, v_words, v_bytes)
            nc.tensor.matmul_mx(
                sums,
                lhsT=w_words[:].bitcast(FP8X4),
                lhsT_scale=w_bytes[:],
                rhs=v_words[:].bitcast(FP8X4),
                rhs_scale=v_bytes[:],
                start=True,
                stop=True,
            )

        def pick2(b):
            tag = f"val_{b - 3}" if b >= 2 else f"negated{b}"
            negated = sb.tile([P, I], F32, name=f"negated{b}", tag=tag, align_bytes=64)
            nc.scalar.activation(negated[:], val2_pool[b][:].indirect(idx3[:]), ACT.Copy, scale=-1.0)
            return negated

        def turn(bank, source, first):
            for r in range(PACK):
                nc.tensor.matmul(
                    bank[:, r, :],
                    lhsT=source[:, r:I:PACK],
                    rhs=ident[:],
                    is_transpose=True,
                    start=(first and r == 0),
                    stop=(not first and r == PACK - 1),
                )

        early_sums = ps.tile([P, 2, P], F32, name="early_sums")
        late_sums = [ps.tile([P, P], F32, name=f"late_sums{j}") for j in range(2)]
        half = I // 2
        negated = pick2(0)
        apart = []
        for b in range(BLOCKS):
            turned = ps.tile([P, PACK, P], F32, name=f"turned{b}", tag=f"turned{b % 2}")
            turn(turned, negated, True)
            picked = sb.tile([P, I], F32, name=f"picked{b}", tag=f"val_{b - 1}", align_bytes=64)
            if b < BLOCKS - 1:
                nc.vector.tensor_copy(picked[:], val_pool[b][:].indirect(idx[:]))
            else:
                nc.vector.tensor_copy(picked[:, :half], val_pool[b][:].indirect(idx[:, : half // 16]))
                nc.scalar.activation(picked[:, half:], val_pool[b][:].indirect(idx[:, half // 16 :]), ACT.Copy)
            turn(turned, picked, False)
            if b < BLOCKS - 1:
                negated = pick2(b + 1)
            apart.append(sb.tile([P, P, PACK], F32, name=f"apart{b}", tag=f"val2_{b + 1}"))
            for cols in halves if b == BLOCKS - 1 else [slice(0, P)]:
                nc.scalar.activation(apart[b][:, cols, :], turned[:, :, cols].rearrange("p r e -> p e r"), ACT.Abs)
            if b == 0:
                scale_and_quantize("w_woven", "val_0", scores[:].rearrange("p r q -> p q r"), os_col, w_words, w_bytes)
            else:
                multiply(b - 1, apart[b - 1], early_sums[:, b - 1, :] if b < BLOCKS - 1 else late_sums[0][:])
            if b == BLOCKS - 2:
                early = sb.tile([P, 2, P], F32, name="early")
                nc.vector.tensor_copy(early[:], early_sums[:])
                nc.sync.dma_start(out[:, : 2 * P], early[:].rearrange("p b e -> p (b e)"))
        multiply(BLOCKS - 1, apart[BLOCKS - 1], late_sums[1][:])
        third = sb.tile([P, P], F32, name="third", tag=f"val2_{BLOCKS}")
        nc.scalar.copy(third[:], late_sums[0][:])
        nc.sync.dma_start(out[:, 2 * P : 3 * P], third[:])
        last = sb.tile([P, P], F32, name="last")
        nc.scalar.copy(last[:], late_sums[1][:])
        nc.scalar.dma_start(out[:, 3 * P :], last[:])
